import numpy as np
import ml_dtypes


def mxq(x, axis, fmt="e4m3"):
    dtype, down = {"e4m3": (ml_dtypes.float8_e4m3fn, 7), "e5m2": (ml_dtypes.float8_e5m2, 14)}[fmt]
    v = np.moveaxis(np.asarray(x, np.float32).astype(ml_dtypes.bfloat16).astype(np.float64), axis, -1)
    blocks = v.reshape(v.shape[:-1] + (-1, 32))
    amax = np.abs(blocks).max(-1, keepdims=True)
    byte = np.maximum(np.where(amax > 0, np.frexp(amax)[1] - 1 + 127, 0) - down, 1)
    scale = np.exp2(byte - 127.0)
    codes = (blocks / scale).astype(np.float32).astype(dtype).astype(np.float64)
    return np.moveaxis((codes * scale).reshape(v.shape), -1, axis)


WIDE = False


def mx_kscale(k):
    if not WIDE:
        return np.ones(k)
    levels = np.array([10, -10, 5, -5, 0])
    if k % 512:
        return np.exp2(np.random.permutation(np.resize(levels, k // 32))).repeat(32)
    a = np.empty((k // 512, 16))
    for p in range(k // 512):
        a[p, :8] = np.random.permutation(np.resize(levels, 8))
        for g in range(8):
            far = levels[np.abs(levels - a[p, g]) >= 10]
            a[p, g + 8] = far[np.random.randint(len(far))]
    return np.exp2(a.ravel()).repeat(32)


def f64(x):
    return np.asarray(x).astype(np.float64)


def striped(idx):
    return np.tile(idx.reshape(-1, 16).T, (8, 1)).astype(np.uint16)


def unstriped(offs):
    return offs[:16].T.reshape(-1).astype(np.int64)


def pack_weight(w):
    k, n = w.shape
    w = f64(np.asarray(w, np.float32).astype(ml_dtypes.bfloat16)).reshape(k // 32, 32, n)
    amax = np.abs(w).max(1)
    byte = np.clip(np.where(amax > 0, np.frexp(amax)[1] - 1 + 127 - 7, 1), 1, 254)
    scaled = (w * np.exp2(127.0 - byte)[:, None, :]).reshape(k, n).astype(np.float32)
    words = np.ascontiguousarray(scaled.reshape(k // 512, 128, 4, n).transpose(0, 1, 3, 2)).astype(ml_dtypes.float8_e4m3fn).view(np.uint8)
    return words, np.ascontiguousarray(byte.astype(np.uint8).reshape(k // 512, 16, n))


def unpack_weight(words, scales):
    g, p, n, _ = words.shape
    vals = np.ascontiguousarray(words).view(ml_dtypes.float8_e4m3fn).astype(np.float64) * np.repeat(np.exp2(scales.astype(np.float64) - 127.0), 8, axis=1)[..., None]
    return vals.transpose(0, 1, 3, 2).reshape(g * 512, n)


K, T, S, N, H = 1024, 2048, 512, 256, 512


def setup_inputs():
    n = np.random.standard_normal
    s = mx_kscale(K)[:, None]
    u = mx_kscale(H)
    packed_xT = pack_weight(n((K, T)) * s)
    return {
        "x_words": packed_xT[0],
        "x_scales": packed_xT[1],
        "w1": (n((K, H)) / np.sqrt(K) / s).astype(np.float32),
        "w2": (n((K, H)) / np.sqrt(K) / s).astype(np.float32),
        "ka": (np.random.uniform(0.6, 1.4, (H, 1))).astype(np.float32),
        "p0": (np.random.uniform(1.0, 1.8, (H, S))).astype(np.float32),
        "unit": (np.random.uniform(0.6, 1.4, (H, 1)) * u[:, None]).astype(np.float32),
        "w3": (n((H, N)) / np.sqrt(H) / u[:, None]).astype(np.float32),
        "offs": striped(np.random.permutation(T)[:S]),
        "nb1": striped(np.random.permutation(S)),
        "nb2": striped(np.random.permutation(S)),
        "nb3": striped(np.random.permutation(S)),
    }


def reference(x_words, x_scales, w1, w2, ka, p0, unit, w3, offs, nb1, nb2, nb3):
    xq = unpack_weight(x_words, x_scales)[:, unstriped(offs)]
    ar = mxq(f64(w2), 0, "e4m3").T @ xq
    area = 0.5 * np.tanh(ar) + 1.2
    press = f64(ka) * (-1.0 * area + 1.0)
    q1 = press[:, unstriped(nb1)]
    q2 = press[:, unstriped(nb2)]
    q3 = press[:, unstriped(nb3)]
    mnb = 0.333 * (q1 + q2 + q3)
    dpr = press - mnb
    pr = mxq(f64(w1), 0, "e4m3").T @ xq
    peri = 0.6 * np.tanh(pr) + 1.5
    tens = 0.8 * (peri - f64(p0))
    hid = f64(unit) * (dpr + tens)
    return mxq(f64(w3), 0, "e4m3").T @ mxq(hid, 0, "e4m3")

@@ -1,0 +1,262 @@
+from contextlib import ExitStack
+
+import concourse.mybir as mybir
+from concourse.masks import make_identity
+
+K, T, S, N, H = 1024, 2048, 512, 256, 512
+FLOPS = 2 * (2 * K * H * S + H * N * S)
+
+F32 = mybir.dt.float32
+BF16 = mybir.dt.bfloat16
+I32 = mybir.dt.int32
+U32 = mybir.dt.uint32
+U16 = mybir.dt.uint16
+U8 = mybir.dt.uint8
+FP8X4 = mybir.dt.float8_e4m3fn_x4
+ALU = mybir.AluOpType
+ACT = mybir.ActivationFunctionType
+
+P = 128
+PACK = 4
+PASSES = K // (P * PACK)
+TILES = H // P
+BLOCKS = S // P
+SPARE = 8
+HALF = S // 2
+TENS = 0.8 * 0.6
+
+
+def tile_picked_yswelt_force_p_kernel(
+    tc, x_words, x_scales, w1, w2, ka, p0, unit, w3, offs, nb1, nb2, nb3, out
+):
+    nc = tc.nc
+    with ExitStack() as ctx:
+        keep = ctx.enter_context(tc.tile_pool(name="keep", bufs=1))
+        psum = ctx.enter_context(tc.psum_pool(name="psum", bufs=1))
+
+        def tile(shape, dtype, name):
+            return keep.tile(shape, dtype, name=name, align_bytes=64)
+
+        def bank(shape, b):
+            return psum.tile(shape, F32, name="bank%d" % b)
+
+        def load_list(src, name):
+            lst = keep.tile([P, S // 16], U16, name=name)
+            nc.sync.dma_start(lst[:], src)
+            return lst
+
+        def load_words(g):
+            words = tile([P, T], I32, "xw%d" % g)
+            nc.sync.dma_start(out=words[:], in_=x_words[g].rearrange("p c r -> p (c r)").bitcast(I32))
+            return words
+
+        def load_rows(w, g, c0, c1, name):
+            raw = tile([P, PACK, c1 - c0], F32, name)
+            rows = w[g * P * PACK:(g + 1) * P * PACK, c0:c1]
+            nc.sync.dma_start(out=raw[:], in_=rows.rearrange("(p j) c -> p j c", j=PACK))
+            return raw
+
+        def load_column(v, name):
+            col = tile([P, TILES], F32, name)
+            with nc.allow_non_contiguous_dma(reason="one value a partition"):
+                nc.sync.dma_start(out=col[:], in_=v.rearrange("(u p) o -> p (u o)", p=P))
+            return col
+
+        xs = tile([P, T], U8, "xs")
+        nc.gpsimd.memset(xs[:].bitcast(I32), 0)
+        ident = tile([P, P], F32, "ident")
+        make_identity(nc, ident[:])
+
+        xw0 = load_words(0)
+        offs_t = load_list(offs, "offs_t")
+        for q in range(4):
+            nc.sync.dma_start(out=xs[32 * q:32 * q + 8, :].bitcast(I32), in_=x_scales[:, 4 * q:4 * q + 4, :].bitcast(I32))
+        xw1 = load_words(1)
+        w2r = {}
+        for u in range(2):
+            for g in range(PASSES):
+                w2r[u, g] = load_rows(w2, g, u * P, (u + 1) * P, "w2r%d%d" % (u, g))
+        ka_t = load_column(ka, "ka_t")
+        nb = {2: load_list(nb3, "nb3_t"), 0: load_list(nb1, "nb1_t")}
+        for g in range(PASSES):
+            w2r[2, g] = load_rows(w2, g, 2 * P, H, "w2r2%d" % g)
+        nb[1] = load_list(nb2, "nb2_t")
+        unit_t = load_column(unit, "unit_t")
+        w1r = [load_rows(w1, g, 0, H, "w1r%d" % g) for g in range(PASSES)]
+        w3r = load_rows(w3, 0, 0, N, "w3r")
+        p0_t = tile([P, TILES, S], F32, "p0_t")
+        nc.sync.dma_start(out=p0_t[:], in_=p0.rearrange("(u p) c -> p u c", p=P))
+
+        def interleave(copy, raw, name):
+            grouped = tile([P, raw.shape[2], PACK], BF16, name)
+            copy(out=grouped[:].rearrange("p (c i) j -> p c j i", i=4), in_=raw[:].rearrange("p j (c i) -> p c j i", i=4))
+            return grouped
+
+        def quantise(grouped, name):
+            width = grouped.shape[1]
+            codes = tile([P, width], U32, name + "c")
+            scales = tile([P, width], U8, name + "s")
+            nc.vector.quantize_mx(out=codes[:].bitcast(FP8X4), scales=scales[:], in_=grouped[:].rearrange("p c j -> p (c j)"))
+            return codes, scales
+
+        xg = [tile([P, S], U32, "xg%d" % g) for g in range(PASSES)]
+        sg = tile([P, S], U8, "sg")
+
+        def product(acc, q, c0, g):
+            nc.tensor.matmul_mx(
+                out=acc[:], lhsT=q[0][:, c0:c0 + P].bitcast(FP8X4), lhsT_scale=q[1][:, c0:c0 + P],
+                rhs=xg[g][:].bitcast(FP8X4), rhs_scale=sg[4 * g:, :], start=(g == 0), stop=(g == PASSES - 1))
+
+        nb_mul = tile([P, TILES], F32, "nb_mul")
+        nb_add = tile([P, TILES], F32, "nb_add")
+        nc.gpsimd.tensor_scalar(nb_mul[:], ka_t[:], 0.5 * 0.333 / TENS, 0.0, ALU.mult, ALU.add)
+        nc.gpsimd.tensor_scalar(nb_add[:], ka_t[:], 0.2 * 0.333 / TENS, 0.0, ALU.mult, ALU.add)
+
+        ta = {}
+        own = {}
+
+        def area(u, q, c0, name):
+            acc = bank([P, S], u)
+            for g in range(PASSES):
+                product(acc, q[g], c0, g)
+            ta[u] = tile([P, S], F32, name)
+            nc.scalar.activation(ta[u][:], acc[:], ACT.Tanh)
+
+        win = {}
+
+        def scale(u, name):
+            win[u] = tile([P, S + SPARE], F32, name)
+            nc.gpsimd.memset(win[u][:, S:], 0.0)
+            nc.vector.tensor_scalar(win[u][:, :S], ta[u][:], nb_mul[:, u:u + 1], nb_add[:, u:u + 1], ALU.mult, ALU.add)
+
+        def own_term(u):
+            own[u] = tile([P, S], F32, "own%d" % u)
+            nc.vector.tensor_scalar(own[u][:], win[u][:, :S], -1.0 / 0.333, 0.8 * 1.5 / TENS, ALU.mult, ALU.add)
+
+        runs = {0: ((0, 1), (2, 3)), 1: ((0, 1), (2,), (3,))}
+        sum_bank = {(0, 0): 2, (0, 1): 3, (1, 0): 0, (1, 1): 1, (1, 2): 4}
+        sums = {}
+
+        def add_term(u, term, halves=(0, 1), last=False):
+            v = u // 2
+            for n, run in enumerate(runs[v]):
+                if run[0] // 2 not in halves:
+                    continue
+                first = (v, n) not in sums
+                if first:
+                    sums[v, n] = bank([P, len(run), 2 * P], sum_bank[v, n])
+                for b, jb in enumerate(run):
+                    c0 = (jb - 2 * halves[0]) * P
+                    nc.tensor.matmul(sums[v, n][:, b, (u % 2) * P:(u % 2 + 1) * P], term[:, c0:c0 + P], ident[:],
+                                     start=(first and b == 0), stop=(last and jb == run[-1]), is_transpose=True)
+
+        def places(i, halves):
+            return nb[i][:, halves[0] * HALF // 16:(halves[-1] + 1) * HALF // 16]
+
+        def fetch(u, i, name, halves=(0, 1)):
+            got = tile([P, HALF * len(halves)], F32, name)
+            nc.scalar.activation(got[:], win[u][:].indirect(places(i, halves)), ACT.Copy)
+            return got[:]
+
+        def fetch_add(u, i, other, name, halves=(0, 1)):
+            got = tile([P, HALF * len(halves)], F32, name)
+            nc.vector.tensor_tensor(got[:], win[u][:].indirect(places(i, halves)), other, ALU.add)
+            return got[:]
+
+        hid_t = [tile([P, 2, H], BF16, "hid%d" % h) for h in range(2)]
+
+        def close(v, n):
+            run = runs[v][n]
+            nc.vector.tensor_tensor(hid_t[run[0] // 2][:, run[0] % 2:run[-1] % 2 + 1, v * 2 * P:(v + 1) * 2 * P], sums[v, n][:],
+                                    unit_row[:, v:v + 1, :].to_broadcast([P, len(run), 2 * P]), ALU.mult)
+
+        def finish(n, back_bank, out_bank, copy_words, copy_out):
+            run = runs[1][n]
+            cols = len(run) * P
+            words = hid_t[run[0] // 2][:].bitcast(F32)
+            back = bank([P, len(run), 2, P], back_bank)
+            for b, jb in enumerate(run):
+                for e in range(2):
+                    nc.tensor.transpose(back[:, b, e, :], words[:, jb % 2, e::2], ident[:])
+            hg = tile([P, cols, PACK], BF16, "hg%d" % n)
+            copy_words(out=hg[:].bitcast(F32).rearrange("p (b r) e -> p b r e", r=P), in_=back[:].rearrange("p b e r -> p b r e"))
+            hc, hs = quantise(hg, "qh%d" % n)
+            acc = bank([P, N // P, cols], out_bank)
+            for mb in range(N // P):
+                nc.tensor.matmul_mx(
+                    out=acc[:, mb, :], lhsT=q3[0][:, mb * P:(mb + 1) * P].bitcast(FP8X4), lhsT_scale=q3[1][:, mb * P:(mb + 1) * P],
+                    rhs=hc[:].bitcast(FP8X4), rhs_scale=hs[:], start=True, stop=True)
+            res = tile([P, N // P, cols], F32, "res%d" % n)
+            copy_out(out=res[:], in_=acc[:])
+            nc.sync.dma_start(out=out[:, run[0] * P:run[0] * P + cols].rearrange("(b p) c -> p b c", p=P), in_=res[:])
+
+        nc.vector.tensor_copy(xg[0][:], xw0[:].bitcast(U32).indirect(offs_t[:]))
+        nc.vector.tensor_copy(sg[:], xs[:].indirect(offs_t[:]))
+        nc.vector.tensor_copy(xg[1][:], xw1[:].bitcast(U32).indirect(offs_t[:]))
+        qq = [[quantise(interleave(nc.scalar.copy, w2r[u, g], "w2g%d%d" % (u, g)), "q2%d%d" % (u, g)) for g in range(PASSES)] for u in range(2)]
+        area(0, qq[0], 0, "w2r11")
+        area(1, qq[1], 0, "ta1")
+        g20 = interleave(nc.vector.tensor_copy, w2r[2, 0], "w2g20")
+        scale(0, "w2r20")
+        q2 = [quantise(g20, "q220")]
+        own_term(0)
+        g21 = interleave(nc.vector.tensor_copy, w2r[2, 1], "w2g21")
+        scale(1, "w2r21")
+        q2.append(quantise(g21, "q221"))
+        own_term(1)
+        area(2, q2, 0, "ta2")
+        area(3, q2, P, "ta3")
+        ub = bank([P, TILES, P], 4)
+        for u in range(TILES):
+            nc.tensor.matmul(ub[:, u, :], unit_t[:, u:u + 1].to_broadcast([P, P]), ident[:], start=True, stop=True, is_transpose=True)
+        f00 = fetch(0, 0, "f00")
+        f01 = fetch(0, 1, "f01")
+        q1 = []
+        for g in range(PASSES):
+            grp = interleave(nc.vector.tensor_copy, w1r[g], "w1g%d" % g)
+            scale(2 + g, "w1r%d" % g)
+            q1.append(quantise(grp, "q1%d" % g))
+            own_term(2 + g)
+        unit_row = tile([P, 2, 2 * P], F32, "q221c")
+        nc.scalar.activation(unit_row[:].rearrange("p v r -> p (v r)"), ub[:].rearrange("p u r -> p (u r)"), ACT.Copy, scale=TENS)
+        f02 = fetch(0, 2, "q221s")
+        add_term(0, own[0][:])
+        add_term(0, f00)
+        add_term(0, f01)
+        acc = [bank([P, S], 4 + u) for u in range(TILES)]
+        for u in range(TILES):
+            for g in range(PASSES):
+                product(acc[u], q1[g], u * P, g)
+        f10 = fetch(1, 0, "ta2")
+        f11 = fetch(1, 1, "f00")
+        f12 = fetch_add(1, 2, own[1][:], "ta3")
+        for u, term in ((1, f12), (0, f02), (1, f11), (1, f10)):
+            add_term(u, term)
+        q3 = quantise(interleave(nc.vector.tensor_copy, w3r, "w3g"), "q3")
+        tension = []
+        for u in range(TILES):
+            tp = tile([P, S], F32, "tp%d" % u)
+            nc.scalar.activation(tp[:], acc[u][:], ACT.Tanh)
+            tension.append(tile([P, S], F32, "tension%d" % u))
+            nc.vector.scalar_tensor_tensor(tension[u][:], p0_t[:, u, :], -0.8 / TENS, tp[:], ALU.mult, ALU.add)
+            add_term(u, tension[u][:], last=(u == 1))
+        add_term(2, fetch(2, 0, "q11c", (0,)), (0,))
+        add_term(2, fetch(2, 1, "q11s", (0,)), (0,))
+        add_term(2, fetch_add(2, 2, own[2][:, :HALF], "tp2", (0,)), (0,))
+        add_term(3, fetch_add(3, 2, own[3][:, :HALF], "tp3", (0,)), (0,))
+        close(0, 0)
+        add_term(3, fetch(3, 0, "tp0", (0,)), (0,))
+        add_term(3, fetch(3, 1, "tp1", (0,)), (0,), last=True)
+        close(1, 0)
+        close(0, 1)
+        add_term(2, fetch(2, 0, "q11c", (1,)), (1,))
+        add_term(2, fetch(2, 1, "q11s", (1,)), (1,))
+        finish(0, 5, 6, nc.scalar.copy, nc.scalar.copy)
+        add_term(2, fetch_add(2, 2, own[2][:, HALF:], "tp2", (1,)), (1,))
+        add_term(3, fetch(3, 0, "tp0", (1,)), (1,))
+        add_term(3, fetch_add(3, 2, own[3][:, HALF:], "tp3", (1,)), (1,))
+        add_term(3, fetch(3, 1, "tp1", (1,)), (1,), last=True)
+        close(1, 1)
+        close(1, 2)
+        finish(1, 2, 3, nc.scalar.copy, nc.scalar.copy)
+        finish(2, 7, 0, nc.vector.tensor_copy, nc.vector.tensor_copy)

@@ -56,36 +56,35 @@ def tile_picked_yswelt_force_p_kernel(
             nc.sync.dma_start(out=raw[:], in_=rows.rearrange("(p j) c -> p j c", j=PACK))
             return raw
 
-        def load_column(v, name):
-            col = tile([P, TILES], F32, name)
-            with nc.allow_non_contiguous_dma(reason="one value a partition"):
-                nc.sync.dma_start(out=col[:], in_=v.rearrange("(u p) o -> p (u o)", p=P))
-            return col
-
         xs = tile([P, T], U8, "xs")
         nc.gpsimd.memset(xs[:].bitcast(I32), 0)
+        rows_t = tile([P, P], F32, "rows_t")
+        nc.gpsimd.memset(rows_t[:], 0.0)
         ident = tile([P, P], F32, "ident")
         make_identity(nc, ident[:])
+        ta = {u: tile([P, S + SPARE], F32, "ta%d" % u) for u in range(TILES)}
+        for u in range(TILES):
+            nc.vector.memset(ta[u][:, S:], 0.0)
 
-        xw0 = load_words(0)
-        offs_t = load_list(offs, "offs_t")
         for q in range(4):
             nc.sync.dma_start(out=xs[32 * q:32 * q + 8, :].bitcast(I32), in_=x_scales[:, 4 * q:4 * q + 4, :].bitcast(I32))
-        xw1 = load_words(1)
+        xw0 = load_words(0)
+        offs_t = load_list(offs, "offs_t")
+        nc.sync.dma_start(out=rows_t[0:TILES, :], in_=ka.rearrange("(u p) o -> u (p o)", p=P))
+        nc.sync.dma_start(out=rows_t[TILES:2 * TILES, :], in_=unit.rearrange("(u p) o -> u (p o)", p=P))
         w2r = {}
-        for u in range(2):
-            for g in range(PASSES):
-                w2r[u, g] = load_rows(w2, g, u * P, (u + 1) * P, "w2r%d%d" % (u, g))
-        ka_t = load_column(ka, "ka_t")
-        nb = {2: load_list(nb3, "nb3_t"), 0: load_list(nb1, "nb1_t")}
+        w2r[0, 0] = load_rows(w2, 0, 0, 2 * P, "w2r00")
+        xw1 = load_words(1)
+        w2r[0, 1] = load_rows(w2, 1, 0, 2 * P, "w2r01")
+        nb = {0: load_list(nb1, "nb1_t"), 1: load_list(nb2, "nb2_t")}
         for g in range(PASSES):
             w2r[2, g] = load_rows(w2, g, 2 * P, H, "w2r2%d" % g)
-        nb[1] = load_list(nb2, "nb2_t")
-        unit_t = load_column(unit, "unit_t")
+        nb[2] = load_list(nb3, "nb3_t")
         w1r = [load_rows(w1, g, 0, H, "w1r%d" % g) for g in range(PASSES)]
         w3r = load_rows(w3, 0, 0, N, "w3r")
-        p0_t = tile([P, TILES, S], F32, "p0_t")
-        nc.sync.dma_start(out=p0_t[:], in_=p0.rearrange("(u p) c -> p u c", p=P))
+        p0_t = [tile([P, 2, S], F32, "p0_t%d" % v) for v in range(2)]
+        for v in range(2):
+            nc.sync.dma_start(out=p0_t[v][:], in_=p0[2 * v * P:2 * (v + 1) * P, :].rearrange("(u p) c -> p u c", p=P))
 
         def interleave(copy, raw, name):
             grouped = tile([P, raw.shape[2], PACK], BF16, name)
@@ -107,27 +106,33 @@ def tile_picked_yswelt_force_p_kernel(
                 out=acc[:], lhsT=q[0][:, c0:c0 + P].bitcast(FP8X4), lhsT_scale=q[1][:, c0:c0 + P],
                 rhs=xg[g][:].bitcast(FP8X4), rhs_scale=sg[4 * g:, :], start=(g == 0), stop=(g == PASSES - 1))
 
+        cols = bank([P, P], 5)
+        nc.tensor.transpose(cols[:], rows_t[:], ident[:])
         nb_mul = tile([P, TILES], F32, "nb_mul")
         nb_add = tile([P, TILES], F32, "nb_add")
-        nc.gpsimd.tensor_scalar(nb_mul[:], ka_t[:], 0.5 * 0.333 / TENS, 0.0, ALU.mult, ALU.add)
-        nc.gpsimd.tensor_scalar(nb_add[:], ka_t[:], 0.2 * 0.333 / TENS, 0.0, ALU.mult, ALU.add)
+        unit_t = tile([P, TILES], F32, "unit_t")
+        nc.scalar.activation(nb_mul[:], cols[:, :TILES], ACT.Copy, scale=0.5 * 0.333 / TENS)
+        nc.scalar.activation(nb_add[:], cols[:, :TILES], ACT.Copy, scale=0.2 * 0.333 / TENS)
+        nc.scalar.activation(unit_t[:], cols[:, TILES:2 * TILES], ACT.Copy, scale=TENS)
+        ub = bank([P, TILES, P], 4)
+        for u in range(TILES):
+            nc.tensor.matmul(ub[:, u, :], unit_t[:, u:u + 1].to_broadcast([P, P]), ident[:], start=True, stop=True, is_transpose=True)
+        unit_row = tile([P, 2, 2 * P], F32, "unit_row")
+        nc.scalar.copy(unit_row[:].rearrange("p v r -> p (v r)"), ub[:].rearrange("p u r -> p (u r)"))
 
-        ta = {}
         own = {}
 
-        def area(u, q, c0, name):
+        def area(u, q, c0):
             acc = bank([P, S], u)
             for g in range(PASSES):
                 product(acc, q[g], c0, g)
-            ta[u] = tile([P, S], F32, name)
-            nc.scalar.activation(ta[u][:], acc[:], ACT.Tanh)
+            nc.scalar.activation(ta[u][:, :S], acc[:], ACT.Tanh)
 
         win = {}
 
         def scale(u, name):
             win[u] = tile([P, S + SPARE], F32, name)
-            nc.gpsimd.memset(win[u][:, S:], 0.0)
-            nc.vector.tensor_scalar(win[u][:, :S], ta[u][:], nb_mul[:, u:u + 1], nb_add[:, u:u + 1], ALU.mult, ALU.add)
+            nc.vector.tensor_scalar(win[u][:], ta[u][:], nb_mul[:, u:u + 1], nb_add[:, u:u + 1], ALU.mult, ALU.add)
 
         def own_term(u):
             own[u] = tile([P, S], F32, "own%d" % u)
@@ -193,9 +198,10 @@ def tile_picked_yswelt_force_p_kernel(
         nc.vector.tensor_copy(xg[0][:], xw0[:].bitcast(U32).indirect(offs_t[:]))
         nc.vector.tensor_copy(sg[:], xs[:].indirect(offs_t[:]))
         nc.vector.tensor_copy(xg[1][:], xw1[:].bitcast(U32).indirect(offs_t[:]))
-        qq = [[quantise(interleave(nc.scalar.copy, w2r[u, g], "w2g%d%d" % (u, g)), "q2%d%d" % (u, g)) for g in range(PASSES)] for u in range(2)]
-        area(0, qq[0], 0, "w2r11")
-        area(1, qq[1], 0, "ta1")
+        q0 = [quantise(interleave(nc.scalar.copy, w2r[0, 0], "w2g00"), "q200"),
+              quantise(interleave(nc.vector.tensor_copy, w2r[0, 1], "w2g01"), "q201")]
+        area(0, q0, 0)
+        area(1, q0, P)
         g20 = interleave(nc.vector.tensor_copy, w2r[2, 0], "w2g20")
         scale(0, "w2r20")
         q2 = [quantise(g20, "q220")]
@@ -204,11 +210,8 @@ def tile_picked_yswelt_force_p_kernel(
         scale(1, "w2r21")
         q2.append(quantise(g21, "q221"))
         own_term(1)
-        area(2, q2, 0, "ta2")
-        area(3, q2, P, "ta3")
-        ub = bank([P, TILES, P], 4)
-        for u in range(TILES):
-            nc.tensor.matmul(ub[:, u, :], unit_t[:, u:u + 1].to_broadcast([P, P]), ident[:], start=True, stop=True, is_transpose=True)
+        area(2, q2, 0)
+        area(3, q2, P)
         f00 = fetch(0, 0, "f00")
         f01 = fetch(0, 1, "f01")
         q1 = []
@@ -217,8 +220,6 @@ def tile_picked_yswelt_force_p_kernel(
             scale(2 + g, "w1r%d" % g)
             q1.append(quantise(grp, "q1%d" % g))
             own_term(2 + g)
-        unit_row = tile([P, 2, 2 * P], F32, "q221c")
-        nc.scalar.activation(unit_row[:].rearrange("p v r -> p (v r)"), ub[:].rearrange("p u r -> p (u r)"), ACT.Copy, scale=TENS)
         f02 = fetch(0, 2, "q221s")
         add_term(0, own[0][:])
         add_term(0, f00)
@@ -230,15 +231,15 @@ def tile_picked_yswelt_force_p_kernel(
         f10 = fetch(1, 0, "ta2")
         f11 = fetch(1, 1, "f00")
         f12 = fetch_add(1, 2, own[1][:], "ta3")
-        for u, term in ((1, f12), (0, f02), (1, f11), (1, f10)):
+        for u, term in ((0, f02), (1, f12), (1, f11), (1, f10)):
             add_term(u, term)
-        q3 = quantise(interleave(nc.vector.tensor_copy, w3r, "w3g"), "q3")
+        q3 = quantise(interleave(nc.scalar.copy, w3r, "w3g"), "q3")
         tension = []
         for u in range(TILES):
             tp = tile([P, S], F32, "tp%d" % u)
             nc.scalar.activation(tp[:], acc[u][:], ACT.Tanh)
             tension.append(tile([P, S], F32, "tension%d" % u))
-            nc.vector.scalar_tensor_tensor(tension[u][:], p0_t[:, u, :], -0.8 / TENS, tp[:], ALU.mult, ALU.add)
+            nc.vector.scalar_tensor_tensor(tension[u][:], p0_t[u // 2][:, u % 2, :], -0.8 / TENS, tp[:], ALU.mult, ALU.add)
             add_term(u, tension[u][:], last=(u == 1))
         add_term(2, fetch(2, 0, "q11c", (0,)), (0,))
         add_term(2, fetch(2, 1, "q11s", (0,)), (0,))

@@ -60,6 +60,8 @@ def tile_picked_yswelt_force_p_kernel(
         nc.gpsimd.memset(xs[:].bitcast(I32), 0)
         rows_t = tile([P, P], F32, "rows_t")
         nc.gpsimd.memset(rows_t[:], 0.0)
+        nc.gpsimd.dma_start(out=rows_t[0:TILES, :], in_=ka.rearrange("(u p) o -> u (p o)", p=P))
+        nc.gpsimd.dma_start(out=rows_t[TILES:2 * TILES, :], in_=unit.rearrange("(u p) o -> u (p o)", p=P))
         ident = tile([P, P], F32, "ident")
         make_identity(nc, ident[:])
         ta = {u: tile([P, S + SPARE], F32, "ta%d" % u) for u in range(TILES)}
@@ -70,8 +72,6 @@ def tile_picked_yswelt_force_p_kernel(
             nc.sync.dma_start(out=xs[32 * q:32 * q + 8, :].bitcast(I32), in_=x_scales[:, 4 * q:4 * q + 4, :].bitcast(I32))
         xw0 = load_words(0)
         offs_t = load_list(offs, "offs_t")
-        nc.sync.dma_start(out=rows_t[0:TILES, :], in_=ka.rearrange("(u p) o -> u (p o)", p=P))
-        nc.sync.dma_start(out=rows_t[TILES:2 * TILES, :], in_=unit.rearrange("(u p) o -> u (p o)", p=P))
         w2r = {}
         w2r[0, 0] = load_rows(w2, 0, 0, 2 * P, "w2r00")
         xw1 = load_words(1)
@@ -88,7 +88,7 @@ def tile_picked_yswelt_force_p_kernel(
 
         def interleave(copy, raw, name):
             grouped = tile([P, raw.shape[2], PACK], BF16, name)
-            copy(out=grouped[:].rearrange("p (c i) j -> p c j i", i=4), in_=raw[:].rearrange("p j (c i) -> p c j i", i=4))
+            copy(out=grouped[:].rearrange("p (c i) j -> p c j i", i=4), in_=raw[:, :, :].rearrange("p j (c i) -> p c j i", i=4))
             return grouped
 
         def quantise(grouped, name):
@@ -198,10 +198,10 @@ def tile_picked_yswelt_force_p_kernel(
         nc.vector.tensor_copy(xg[0][:], xw0[:].bitcast(U32).indirect(offs_t[:]))
         nc.vector.tensor_copy(sg[:], xs[:].indirect(offs_t[:]))
         nc.vector.tensor_copy(xg[1][:], xw1[:].bitcast(U32).indirect(offs_t[:]))
-        q0 = [quantise(interleave(nc.scalar.copy, w2r[0, 0], "w2g00"), "q200"),
-              quantise(interleave(nc.vector.tensor_copy, w2r[0, 1], "w2g01"), "q201")]
-        area(0, q0, 0)
-        area(1, q0, P)
+        q00 = quantise(interleave(nc.scalar.copy, w2r[0, 0], "w2g00"), "q200")
+        for u, copy in enumerate((nc.vector.tensor_copy, nc.scalar.copy)):
+            q01 = quantise(interleave(copy, w2r[0, 1][:, :, u * P:(u + 1) * P], "w2g01%d" % u), "q201%d" % u)
+            area(u, [(q00[0][:, u * P:], q00[1][:, u * P:]), q01], 0)
         g20 = interleave(nc.vector.tensor_copy, w2r[2, 0], "w2g20")
         scale(0, "w2r20")
         q2 = [quantise(g20, "q220")]

@@ -20,10 +20,15 @@ P = 128
 PACK = 4
 PASSES = K // (P * PACK)
 TILES = H // P
-BLOCKS = S // P
-SPARE = 8
+PAIR = 2 * P
 HALF = S // 2
+PER_COLUMN = 16
+SPARE = 8
 TENS = 0.8 * 0.6
+
+RUNS = {0: ((0, 1), (2, 3)), 1: ((0, 1), (2,), (3,))}
+SUM_BANK = {(0, 0): 2, (0, 1): 3, (1, 0): 0, (1, 1): 1, (1, 2): 4}
+FIRST_HALF, SECOND_HALF, BOTH_HALVES = (0,), (1,), (0, 1)
 
 
 def tile_picked_yswelt_force_p_kernel(
@@ -34,230 +39,228 @@ def tile_picked_yswelt_force_p_kernel(
         keep = ctx.enter_context(tc.tile_pool(name="keep", bufs=1))
         psum = ctx.enter_context(tc.psum_pool(name="psum", bufs=1))
 
-        def tile(shape, dtype, name):
-            return keep.tile(shape, dtype, name=name, align_bytes=64)
+        def tile(shape, dtype, name, on=""):
+            return keep.tile(shape, dtype, name=name, tag=on, align_bytes=64)
 
         def bank(shape, b):
             return psum.tile(shape, F32, name="bank%d" % b)
 
         def load_list(src, name):
-            lst = keep.tile([P, S // 16], U16, name=name)
-            nc.sync.dma_start(lst[:], src)
-            return lst
+            entries = keep.tile([P, S // PER_COLUMN], U16, name=name)
+            nc.sync.dma_start(entries[:], src)
+            return entries
 
         def load_words(g):
-            words = tile([P, T], I32, "xw%d" % g)
+            words = tile([P, T], I32, "x_words%d" % g)
             nc.sync.dma_start(out=words[:], in_=x_words[g].rearrange("p c r -> p (c r)").bitcast(I32))
             return words
 
         def load_rows(w, g, c0, c1, name):
             raw = tile([P, PACK, c1 - c0], F32, name)
             rows = w[g * P * PACK:(g + 1) * P * PACK, c0:c1]
-            nc.sync.dma_start(out=raw[:], in_=rows.rearrange("(p j) c -> p j c", j=PACK))
+            nc.sync.dma_start(out=raw[:], in_=rows.rearrange("(p t) c -> p t c", t=PACK))
             return raw
 
-        xs = tile([P, T], U8, "xs")
-        nc.gpsimd.memset(xs[:].bitcast(I32), 0)
-        rows_t = tile([P, P], F32, "rows_t")
-        nc.gpsimd.memset(rows_t[:], 0.0)
-        nc.gpsimd.dma_start(out=rows_t[0:TILES, :], in_=ka.rearrange("(u p) o -> u (p o)", p=P))
-        nc.gpsimd.dma_start(out=rows_t[TILES:2 * TILES, :], in_=unit.rearrange("(u p) o -> u (p o)", p=P))
+        x_planes = tile([P, T], U8, "x_planes")
+        nc.gpsimd.memset(x_planes[:].bitcast(I32), 0)
+        factor_rows = tile([P, P], F32, "factor_rows")
+        nc.gpsimd.memset(factor_rows[:], 0.0)
         ident = tile([P, P], F32, "ident")
         make_identity(nc, ident[:])
-        ta = {u: tile([P, S + SPARE], F32, "ta%d" % u) for u in range(TILES)}
+        tanh_ar = [tile([P, S + SPARE], F32, "tanh_ar%d" % u) for u in range(TILES)]
         for u in range(TILES):
-            nc.vector.memset(ta[u][:, S:], 0.0)
+            nc.vector.memset(tanh_ar[u][:, S:], 0.0)
 
         for q in range(4):
-            nc.sync.dma_start(out=xs[32 * q:32 * q + 8, :].bitcast(I32), in_=x_scales[:, 4 * q:4 * q + 4, :].bitcast(I32))
-        xw0 = load_words(0)
-        offs_t = load_list(offs, "offs_t")
-        w2r = {}
-        w2r[0, 0] = load_rows(w2, 0, 0, 2 * P, "w2r00")
-        xw1 = load_words(1)
-        w2r[0, 1] = load_rows(w2, 1, 0, 2 * P, "w2r01")
-        nb = {0: load_list(nb1, "nb1_t"), 1: load_list(nb2, "nb2_t")}
+            nc.sync.dma_start(out=x_planes[32 * q:32 * q + 4 * PASSES, :].bitcast(I32),
+                              in_=x_scales[:, 4 * q:4 * q + 4, :].bitcast(I32))
+        x_table = [load_words(0)]
+        picked = load_list(offs, "picked")
+        w2_raw = {(0, 0): load_rows(w2, 0, 0, PAIR, "w2_raw00")}
+        x_table.append(load_words(1))
+        nc.sync.dma_start(out=factor_rows[0:TILES, :], in_=ka.rearrange("(u p) o -> u (p o)", p=P))
+        nc.sync.dma_start(out=factor_rows[TILES:2 * TILES, :], in_=unit.rearrange("(u p) o -> u (p o)", p=P))
+        w2_raw[0, 1] = load_rows(w2, 1, 0, PAIR, "w2_raw01")
+        neighbours = [load_list(nb1, "nb1_list"), load_list(nb2, "nb2_list")]
         for g in range(PASSES):
-            w2r[2, g] = load_rows(w2, g, 2 * P, H, "w2r2%d" % g)
-        nb[2] = load_list(nb3, "nb3_t")
-        w1r = [load_rows(w1, g, 0, H, "w1r%d" % g) for g in range(PASSES)]
-        w3r = load_rows(w3, 0, 0, N, "w3r")
-        p0_t = [tile([P, 2, S], F32, "p0_t%d" % v) for v in range(2)]
+            w2_raw[1, g] = load_rows(w2, g, PAIR, H, "w2_raw1%d" % g)
+        neighbours.append(load_list(nb3, "nb3_list"))
+        w1_raw = [load_rows(w1, g, 0, H, "w1_raw%d" % g) for g in range(PASSES)]
+        w3_raw = load_rows(w3, 0, 0, N, "w3_raw")
+        p0_pair = [tile([P, 2, S], F32, "p0_pair%d" % v) for v in range(2)]
         for v in range(2):
-            nc.sync.dma_start(out=p0_t[v][:], in_=p0[2 * v * P:2 * (v + 1) * P, :].rearrange("(u p) c -> p u c", p=P))
+            nc.sync.dma_start(out=p0_pair[v][:], in_=p0[v * PAIR:(v + 1) * PAIR, :].rearrange("(r p) c -> p r c", p=P))
 
         def interleave(copy, raw, name):
             grouped = tile([P, raw.shape[2], PACK], BF16, name)
-            copy(out=grouped[:].rearrange("p (c i) j -> p c j i", i=4), in_=raw[:, :, :].rearrange("p j (c i) -> p c j i", i=4))
+            copy(out=grouped[:].rearrange("p (c i) t -> p c t i", i=4),
+                 in_=raw[:, :, :].rearrange("p t (c i) -> p c t i", i=4))
             return grouped
 
         def quantise(grouped, name):
             width = grouped.shape[1]
-            codes = tile([P, width], U32, name + "c")
-            scales = tile([P, width], U8, name + "s")
-            nc.vector.quantize_mx(out=codes[:].bitcast(FP8X4), scales=scales[:], in_=grouped[:].rearrange("p c j -> p (c j)"))
+            codes = tile([P, width], U32, name + "_codes")
+            scales = tile([P, width], U8, name + "_scales")
+            nc.vector.quantize_mx(out=codes[:].bitcast(FP8X4), scales=scales[:],
+                                  in_=grouped[:].rearrange("p c t -> p (c t)"))
             return codes, scales
 
-        xg = [tile([P, S], U32, "xg%d" % g) for g in range(PASSES)]
-        sg = tile([P, S], U8, "sg")
+        x_codes = [tile([P, S], U32, "x_codes%d" % g) for g in range(PASSES)]
+        x_bytes = tile([P, S], U8, "x_bytes")
 
-        def product(acc, q, c0, g):
+        def product(acc, weights, c0, g):
+            codes, scales = weights
             nc.tensor.matmul_mx(
-                out=acc[:], lhsT=q[0][:, c0:c0 + P].bitcast(FP8X4), lhsT_scale=q[1][:, c0:c0 + P],
-                rhs=xg[g][:].bitcast(FP8X4), rhs_scale=sg[4 * g:, :], start=(g == 0), stop=(g == PASSES - 1))
+                out=acc[:], lhsT=codes[:, c0:c0 + P].bitcast(FP8X4), lhsT_scale=scales[:, c0:c0 + P],
+                rhs=x_codes[g][:].bitcast(FP8X4), rhs_scale=x_bytes[4 * g:, :], start=(g == 0), stop=(g == PASSES - 1))
 
-        cols = bank([P, P], 5)
-        nc.tensor.transpose(cols[:], rows_t[:], ident[:])
-        nb_mul = tile([P, TILES], F32, "nb_mul")
-        nb_add = tile([P, TILES], F32, "nb_add")
-        unit_t = tile([P, TILES], F32, "unit_t")
-        nc.scalar.activation(nb_mul[:], cols[:, :TILES], ACT.Copy, scale=0.5 * 0.333 / TENS)
-        nc.scalar.activation(nb_add[:], cols[:, :TILES], ACT.Copy, scale=0.2 * 0.333 / TENS)
-        nc.scalar.activation(unit_t[:], cols[:, TILES:2 * TILES], ACT.Copy, scale=TENS)
-        ub = bank([P, TILES, P], 4)
+        factor_cols = bank([P, P], 5)
+        nc.tensor.transpose(factor_cols[:], factor_rows[:], ident[:])
+        near_mul = tile([P, TILES], F32, "near_mul")
+        near_add = tile([P, TILES], F32, "near_add")
+        unit_col = tile([P, TILES], F32, "unit_col")
+        nc.scalar.activation(near_mul[:], factor_cols[:, :TILES], ACT.Copy, scale=0.5 * 0.333 / TENS)
+        nc.scalar.activation(near_add[:], factor_cols[:, :TILES], ACT.Copy, scale=0.2 * 0.333 / TENS)
+        nc.scalar.activation(unit_col[:], factor_cols[:, TILES:2 * TILES], ACT.Copy, scale=TENS)
+        unit_spread = bank([P, TILES, P], 4)
         for u in range(TILES):
-            nc.tensor.matmul(ub[:, u, :], unit_t[:, u:u + 1].to_broadcast([P, P]), ident[:], start=True, stop=True, is_transpose=True)
-        unit_row = tile([P, 2, 2 * P], F32, "unit_row")
-        nc.scalar.copy(unit_row[:].rearrange("p v r -> p (v r)"), ub[:].rearrange("p u r -> p (u r)"))
+            nc.tensor.matmul(unit_spread[:, u, :], unit_col[:, u:u + 1].to_broadcast([P, P]), ident[:],
+                             start=True, stop=True, is_transpose=True)
 
-        own = {}
+        near, own, sums = {}, {}, {}
 
-        def area(u, q, c0):
+        def area(u, weights, c0):
             acc = bank([P, S], u)
             for g in range(PASSES):
-                product(acc, q[g], c0, g)
-            nc.scalar.activation(ta[u][:, :S], acc[:], ACT.Tanh)
+                product(acc, weights[g], c0, g)
+            nc.scalar.activation(tanh_ar[u][:, :S], acc[:], ACT.Tanh)
 
-        win = {}
+        def make_near(u, on):
+            near[u] = tile([P, S + SPARE], F32, "near%d" % u, on)
+            nc.vector.tensor_scalar(near[u][:], tanh_ar[u][:], near_mul[:, u:u + 1], near_add[:, u:u + 1], ALU.mult, ALU.add)
 
-        def scale(u, name):
-            win[u] = tile([P, S + SPARE], F32, name)
-            nc.vector.tensor_scalar(win[u][:], ta[u][:], nb_mul[:, u:u + 1], nb_add[:, u:u + 1], ALU.mult, ALU.add)
-
-        def own_term(u):
+        def make_own(u):
             own[u] = tile([P, S], F32, "own%d" % u)
-            nc.vector.tensor_scalar(own[u][:], win[u][:, :S], -1.0 / 0.333, 0.8 * 1.5 / TENS, ALU.mult, ALU.add)
+            nc.vector.tensor_scalar(own[u][:], near[u][:, :S], -1.0 / 0.333, 0.8 * 1.5 / TENS, ALU.mult, ALU.add)
 
-        runs = {0: ((0, 1), (2, 3)), 1: ((0, 1), (2,), (3,))}
-        sum_bank = {(0, 0): 2, (0, 1): 3, (1, 0): 0, (1, 1): 1, (1, 2): 4}
-        sums = {}
-
-        def add_term(u, term, halves=(0, 1), last=False):
+        def add_term(u, term, halves=BOTH_HALVES, last=False):
             v = u // 2
-            for n, run in enumerate(runs[v]):
+            for n, run in enumerate(RUNS[v]):
                 if run[0] // 2 not in halves:
                     continue
                 first = (v, n) not in sums
                 if first:
-                    sums[v, n] = bank([P, len(run), 2 * P], sum_bank[v, n])
+                    sums[v, n] = bank([P, len(run), PAIR], SUM_BANK[v, n])
                 for b, jb in enumerate(run):
                     c0 = (jb - 2 * halves[0]) * P
                     nc.tensor.matmul(sums[v, n][:, b, (u % 2) * P:(u % 2 + 1) * P], term[:, c0:c0 + P], ident[:],
                                      start=(first and b == 0), stop=(last and jb == run[-1]), is_transpose=True)
 
-        def places(i, halves):
-            return nb[i][:, halves[0] * HALF // 16:(halves[-1] + 1) * HALF // 16]
+        def looked_up(u, i, halves):
+            entries = neighbours[i][:, halves[0] * HALF // PER_COLUMN:(halves[-1] + 1) * HALF // PER_COLUMN]
+            return near[u][:].indirect(entries)
 
-        def fetch(u, i, name, halves=(0, 1)):
-            got = tile([P, HALF * len(halves)], F32, name)
-            nc.scalar.activation(got[:], win[u][:].indirect(places(i, halves)), ACT.Copy)
+        def fetch(u, i, halves=BOTH_HALVES, on=""):
+            got = tile([P, HALF * len(halves)], F32, "got%d%d" % (u, i), on)
+            nc.scalar.activation(got[:], looked_up(u, i, halves), ACT.Copy)
             return got[:]
 
-        def fetch_add(u, i, other, name, halves=(0, 1)):
-            got = tile([P, HALF * len(halves)], F32, name)
-            nc.vector.tensor_tensor(got[:], win[u][:].indirect(places(i, halves)), other, ALU.add)
+        def fetch_with_own(u, halves=BOTH_HALVES, on=""):
+            got = tile([P, HALF * len(halves)], F32, "got%d2" % u, on)
+            plain = own[u][:, halves[0] * HALF:(halves[-1] + 1) * HALF]
+            nc.vector.tensor_tensor(got[:], looked_up(u, 2, halves), plain, ALU.add)
             return got[:]
 
-        hid_t = [tile([P, 2, H], BF16, "hid%d" % h) for h in range(2)]
+        hid_turned = [tile([P, 2, H], BF16, "hid_turned%d" % h) for h in range(2)]
 
         def close(v, n):
-            run = runs[v][n]
-            nc.vector.tensor_tensor(hid_t[run[0] // 2][:, run[0] % 2:run[-1] % 2 + 1, v * 2 * P:(v + 1) * 2 * P], sums[v, n][:],
-                                    unit_row[:, v:v + 1, :].to_broadcast([P, len(run), 2 * P]), ALU.mult)
+            run = RUNS[v][n]
+            nc.vector.tensor_tensor(hid_turned[run[0] // 2][:, run[0] % 2:run[-1] % 2 + 1, v * PAIR:(v + 1) * PAIR],
+                                    sums[v, n][:], unit_row[:, v:v + 1, :].to_broadcast([P, len(run), PAIR]), ALU.mult)
 
-        def finish(n, back_bank, out_bank, copy_words, copy_out):
-            run = runs[1][n]
-            cols = len(run) * P
-            words = hid_t[run[0] // 2][:].bitcast(F32)
+        def finish(n, back_bank, out_bank, copy):
+            run = RUNS[1][n]
+            cells = len(run) * P
+            words = hid_turned[run[0] // 2][:].bitcast(F32)
             back = bank([P, len(run), 2, P], back_bank)
             for b, jb in enumerate(run):
                 for e in range(2):
                     nc.tensor.transpose(back[:, b, e, :], words[:, jb % 2, e::2], ident[:])
-            hg = tile([P, cols, PACK], BF16, "hg%d" % n)
-            copy_words(out=hg[:].bitcast(F32).rearrange("p (b r) e -> p b r e", r=P), in_=back[:].rearrange("p b e r -> p b r e"))
-            hc, hs = quantise(hg, "qh%d" % n)
-            acc = bank([P, N // P, cols], out_bank)
-            for mb in range(N // P):
+            grouped = tile([P, cells, PACK], BF16, "hid_grouped%d" % n)
+            copy(out=grouped[:].bitcast(F32).rearrange("p (b c) e -> p b c e", c=P), in_=back[:].rearrange("p b e c -> p b c e"))
+            codes, scales = quantise(grouped, "hid%d" % n)
+            acc = bank([P, N // P, cells], out_bank)
+            for m in range(N // P):
                 nc.tensor.matmul_mx(
-                    out=acc[:, mb, :], lhsT=q3[0][:, mb * P:(mb + 1) * P].bitcast(FP8X4), lhsT_scale=q3[1][:, mb * P:(mb + 1) * P],
-                    rhs=hc[:].bitcast(FP8X4), rhs_scale=hs[:], start=True, stop=True)
-            res = tile([P, N // P, cols], F32, "res%d" % n)
-            copy_out(out=res[:], in_=acc[:])
-            nc.sync.dma_start(out=out[:, run[0] * P:run[0] * P + cols].rearrange("(b p) c -> p b c", p=P), in_=res[:])
+                    out=acc[:, m, :], lhsT=w3_q[0][:, m * P:(m + 1) * P].bitcast(FP8X4), lhsT_scale=w3_q[1][:, m * P:(m + 1) * P],
+                    rhs=codes[:].bitcast(FP8X4), rhs_scale=scales[:], start=True, stop=True)
+            result = tile([P, N // P, cells], F32, "result%d" % n)
+            copy(out=result[:], in_=acc[:])
+            nc.sync.dma_start(out=out[:, run[0] * P:run[0] * P + cells].rearrange("(m p) c -> p m c", p=P), in_=result[:])
 
-        nc.vector.tensor_copy(xg[0][:], xw0[:].bitcast(U32).indirect(offs_t[:]))
-        nc.vector.tensor_copy(sg[:], xs[:].indirect(offs_t[:]))
-        nc.vector.tensor_copy(xg[1][:], xw1[:].bitcast(U32).indirect(offs_t[:]))
-        q00 = quantise(interleave(nc.scalar.copy, w2r[0, 0], "w2g00"), "q200")
+        nc.vector.tensor_copy(x_codes[0][:], x_table[0][:].bitcast(U32).indirect(picked[:]))
+        nc.vector.tensor_copy(x_bytes[:], x_planes[:].indirect(picked[:]))
+        nc.vector.tensor_copy(x_codes[1][:], x_table[1][:].bitcast(U32).indirect(picked[:]))
+        codes, scales = quantise(interleave(nc.scalar.copy, w2_raw[0, 0], "w2_grouped00"), "w2_00")
         for u, copy in enumerate((nc.vector.tensor_copy, nc.scalar.copy)):
-            q01 = quantise(interleave(copy, w2r[0, 1][:, :, u * P:(u + 1) * P], "w2g01%d" % u), "q201%d" % u)
-            area(u, [(q00[0][:, u * P:], q00[1][:, u * P:]), q01], 0)
-        g20 = interleave(nc.vector.tensor_copy, w2r[2, 0], "w2g20")
-        scale(0, "w2r20")
-        q2 = [quantise(g20, "q220")]
-        own_term(0)
-        g21 = interleave(nc.vector.tensor_copy, w2r[2, 1], "w2g21")
-        scale(1, "w2r21")
-        q2.append(quantise(g21, "q221"))
-        own_term(1)
-        area(2, q2, 0)
-        area(3, q2, P)
-        f00 = fetch(0, 0, "f00")
-        f01 = fetch(0, 1, "f01")
-        q1 = []
+            second = quantise(interleave(copy, w2_raw[0, 1][:, :, u * P:(u + 1) * P], "w2_grouped01%d" % u), "w2_01%d" % u)
+            area(u, [(codes[:, u * P:], scales[:, u * P:]), second], 0)
+        unit_row = tile([P, 2, PAIR], F32, "unit_row", on="w2_raw01")
+        nc.scalar.copy(unit_row[:].rearrange("p v r -> p (v r)"), unit_spread[:].rearrange("p u r -> p (u r)"))
+
+        w2_q, w1_q = [], []
         for g in range(PASSES):
-            grp = interleave(nc.vector.tensor_copy, w1r[g], "w1g%d" % g)
-            scale(2 + g, "w1r%d" % g)
-            q1.append(quantise(grp, "q1%d" % g))
-            own_term(2 + g)
-        f02 = fetch(0, 2, "q221s")
-        add_term(0, own[0][:])
-        add_term(0, f00)
-        add_term(0, f01)
-        acc = [bank([P, S], 4 + u) for u in range(TILES)]
+            grouped = interleave(nc.vector.tensor_copy, w2_raw[1, g], "w2_grouped1%d" % g)
+            make_near(g, on="w2_raw1%d" % g)
+            w2_q.append(quantise(grouped, "w2_1%d" % g))
+            make_own(g)
+        area(2, w2_q, 0)
+        area(3, w2_q, P)
+        got00 = fetch(0, 0)
+        got01 = fetch(0, 1)
+        for g in range(PASSES):
+            grouped = interleave(nc.vector.tensor_copy, w1_raw[g], "w1_grouped%d" % g)
+            make_near(2 + g, on="w1_raw%d" % g)
+            w1_q.append(quantise(grouped, "w1_%d" % g))
+            make_own(2 + g)
+
+        got02 = fetch(0, 2, on="w2_11_scales")
+        for term in (own[0][:], got00, got01):
+            add_term(0, term)
+        pr = [bank([P, S], TILES + u) for u in range(TILES)]
         for u in range(TILES):
             for g in range(PASSES):
-                product(acc[u], q1[g], u * P, g)
-        f10 = fetch(1, 0, "ta2")
-        f11 = fetch(1, 1, "f00")
-        f12 = fetch_add(1, 2, own[1][:], "ta3")
-        for u, term in ((0, f02), (1, f12), (1, f11), (1, f10)):
+                product(pr[u], w1_q[g], u * P, g)
+        got10 = fetch(1, 0, on="tanh_ar2")
+        got11 = fetch(1, 1, on="got00")
+        got12 = fetch_with_own(1, on="tanh_ar3")
+        for u, term in ((0, got02), (1, got12), (1, got11), (1, got10)):
             add_term(u, term)
-        q3 = quantise(interleave(nc.scalar.copy, w3r, "w3g"), "q3")
-        tension = []
+        w3_q = quantise(interleave(nc.scalar.copy, w3_raw, "w3_grouped"), "w3")
         for u in range(TILES):
-            tp = tile([P, S], F32, "tp%d" % u)
-            nc.scalar.activation(tp[:], acc[u][:], ACT.Tanh)
-            tension.append(tile([P, S], F32, "tension%d" % u))
-            nc.vector.scalar_tensor_tensor(tension[u][:], p0_t[u // 2][:, u % 2, :], -0.8 / TENS, tp[:], ALU.mult, ALU.add)
-            add_term(u, tension[u][:], last=(u == 1))
-        add_term(2, fetch(2, 0, "q11c", (0,)), (0,))
-        add_term(2, fetch(2, 1, "q11s", (0,)), (0,))
-        add_term(2, fetch_add(2, 2, own[2][:, :HALF], "tp2", (0,)), (0,))
-        add_term(3, fetch_add(3, 2, own[3][:, :HALF], "tp3", (0,)), (0,))
+            tanh_pr = tile([P, S], F32, "tanh_pr%d" % u)
+            nc.scalar.activation(tanh_pr[:], pr[u][:], ACT.Tanh)
+            tension = tile([P, S], F32, "tension%d" % u)
+            nc.vector.scalar_tensor_tensor(tension[:], p0_pair[u // 2][:, u % 2, :], -0.8 / TENS, tanh_pr[:], ALU.mult, ALU.add)
+            add_term(u, tension[:], last=(u == 1))
+
+        add_term(2, fetch(2, 0, FIRST_HALF, on="w1_1_codes"), FIRST_HALF)
+        add_term(2, fetch(2, 1, FIRST_HALF, on="w1_1_scales"), FIRST_HALF)
+        add_term(2, fetch_with_own(2, FIRST_HALF, on="tanh_pr2"), FIRST_HALF)
+        add_term(3, fetch_with_own(3, FIRST_HALF, on="tanh_pr3"), FIRST_HALF)
         close(0, 0)
-        add_term(3, fetch(3, 0, "tp0", (0,)), (0,))
-        add_term(3, fetch(3, 1, "tp1", (0,)), (0,), last=True)
+        add_term(3, fetch(3, 0, FIRST_HALF, on="tanh_pr0"), FIRST_HALF)
+        add_term(3, fetch(3, 1, FIRST_HALF, on="tanh_pr1"), FIRST_HALF, last=True)
         close(1, 0)
         close(0, 1)
-        add_term(2, fetch(2, 0, "q11c", (1,)), (1,))
-        add_term(2, fetch(2, 1, "q11s", (1,)), (1,))
-        finish(0, 5, 6, nc.scalar.copy, nc.scalar.copy)
-        add_term(2, fetch_add(2, 2, own[2][:, HALF:], "tp2", (1,)), (1,))
-        add_term(3, fetch(3, 0, "tp0", (1,)), (1,))
-        add_term(3, fetch_add(3, 2, own[3][:, HALF:], "tp3", (1,)), (1,))
-        add_term(3, fetch(3, 1, "tp1", (1,)), (1,), last=True)
+        add_term(2, fetch(2, 0, SECOND_HALF, on="w1_1_codes"), SECOND_HALF)
+        add_term(2, fetch(2, 1, SECOND_HALF, on="w1_1_scales"), SECOND_HALF)
+        finish(0, back_bank=5, out_bank=6, copy=nc.scalar.copy)
+        add_term(2, fetch_with_own(2, SECOND_HALF, on="tanh_pr2"), SECOND_HALF)
+        add_term(3, fetch(3, 0, SECOND_HALF, on="tanh_pr0"), SECOND_HALF)
+        add_term(3, fetch_with_own(3, SECOND_HALF, on="tanh_pr3"), SECOND_HALF)
+        add_term(3, fetch(3, 1, SECOND_HALF, on="tanh_pr1"), SECOND_HALF, last=True)
         close(1, 1)
         close(1, 2)
-        finish(1, 2, 3, nc.scalar.copy, nc.scalar.copy)
-        finish(2, 7, 0, nc.vector.tensor_copy, nc.vector.tensor_copy)
+        finish(1, back_bank=2, out_bank=3, copy=nc.scalar.copy)
+        finish(2, back_bank=7, out_bank=0, copy=nc.vector.tensor_copy)

@@ -63,23 +63,23 @@ def tile_picked_yswelt_force_p_kernel(
 
         x_planes = tile([P, T], U8, "x_planes")
         nc.gpsimd.memset(x_planes[:].bitcast(I32), 0)
-        factor_rows = tile([P, P], F32, "factor_rows")
-        nc.gpsimd.memset(factor_rows[:], 0.0)
         ident = tile([P, P], F32, "ident")
         make_identity(nc, ident[:])
         tanh_ar = [tile([P, S + SPARE], F32, "tanh_ar%d" % u) for u in range(TILES)]
         for u in range(TILES):
             nc.vector.memset(tanh_ar[u][:, S:], 0.0)
 
+        factor_rows = tile([P, P], F32, "factor_rows")
+        for n, factor in enumerate((ka, unit)):
+            rows = factor.rearrange("(u p) o -> o u p", p=P).to_broadcast([P // 2 // TILES, TILES, P])
+            nc.sync.dma_start(out=factor_rows[n * P // 2:(n + 1) * P // 2, :], in_=rows)
+        x_table = [load_words(0)]
+        picked = load_list(offs, "picked")
         for q in range(4):
             nc.sync.dma_start(out=x_planes[32 * q:32 * q + 4 * PASSES, :].bitcast(I32),
                               in_=x_scales[:, 4 * q:4 * q + 4, :].bitcast(I32))
-        x_table = [load_words(0)]
-        picked = load_list(offs, "picked")
         w2_raw = {(0, 0): load_rows(w2, 0, 0, PAIR, "w2_raw00")}
         x_table.append(load_words(1))
-        nc.sync.dma_start(out=factor_rows[0:TILES, :], in_=ka.rearrange("(u p) o -> u (p o)", p=P))
-        nc.sync.dma_start(out=factor_rows[TILES:2 * TILES, :], in_=unit.rearrange("(u p) o -> u (p o)", p=P))
         w2_raw[0, 1] = load_rows(w2, 1, 0, PAIR, "w2_raw01")
         neighbours = [load_list(nb1, "nb1_list"), load_list(nb2, "nb2_list")]
         for g in range(PASSES):
@@ -121,11 +121,13 @@ def tile_picked_yswelt_force_p_kernel(
         unit_col = tile([P, TILES], F32, "unit_col")
         nc.scalar.activation(near_mul[:], factor_cols[:, :TILES], ACT.Copy, scale=0.5 * 0.333 / TENS)
         nc.scalar.activation(near_add[:], factor_cols[:, :TILES], ACT.Copy, scale=0.2 * 0.333 / TENS)
-        nc.scalar.activation(unit_col[:], factor_cols[:, TILES:2 * TILES], ACT.Copy, scale=TENS)
+        nc.scalar.activation(unit_col[:], factor_cols[:, P // 2:P // 2 + TILES], ACT.Copy, scale=TENS)
         unit_spread = bank([P, TILES, P], 4)
         for u in range(TILES):
             nc.tensor.matmul(unit_spread[:, u, :], unit_col[:, u:u + 1].to_broadcast([P, P]), ident[:],
                              start=True, stop=True, is_transpose=True)
+        unit_row = tile([P, 2, PAIR], F32, "unit_row")
+        nc.scalar.copy(unit_row[:].rearrange("p v r -> p (v r)"), unit_spread[:].rearrange("p u r -> p (u r)"))
 
         near, own, sums = {}, {}, {}
 
@@ -205,8 +207,6 @@ def tile_picked_yswelt_force_p_kernel(
         for u, copy in enumerate((nc.vector.tensor_copy, nc.scalar.copy)):
             second = quantise(interleave(copy, w2_raw[0, 1][:, :, u * P:(u + 1) * P], "w2_grouped01%d" % u), "w2_01%d" % u)
             area(u, [(codes[:, u * P:], scales[:, u * P:]), second], 0)
-        unit_row = tile([P, 2, PAIR], F32, "unit_row", on="w2_raw01")
-        nc.scalar.copy(unit_row[:].rearrange("p v r -> p (v r)"), unit_spread[:].rearrange("p u r -> p (u r)"))
 
         w2_q, w1_q = [], []
         for g in range(PASSES):

from contextlib import ExitStack

import concourse.mybir as mybir
from concourse.masks import make_identity

K, T, S, N, H = 1024, 2048, 512, 256, 512
FLOPS = 2 * (2 * K * H * S + H * N * S)

F32 = mybir.dt.float32
BF16 = mybir.dt.bfloat16
I32 = mybir.dt.int32
U32 = mybir.dt.uint32
U16 = mybir.dt.uint16
U8 = mybir.dt.uint8
FP8X4 = mybir.dt.float8_e4m3fn_x4
ALU = mybir.AluOpType
ACT = mybir.ActivationFunctionType

P = 128
PACK = 4
PASSES = K // (P * PACK)
TILES = H // P
PAIR = 2 * P
HALF = S // 2
PER_COLUMN = 16
SPARE = 8
TENS = 0.8 * 0.6

RUNS = {0: ((0, 1), (2, 3)), 1: ((0, 1), (2,), (3,))}
SUM_BANK = {(0, 0): 2, (0, 1): 3, (1, 0): 0, (1, 1): 1, (1, 2): 4}
FIRST_HALF, SECOND_HALF, BOTH_HALVES = (0,), (1,), (0, 1)


def tile_picked_yswelt_force_p_kernel(
    tc, x_words, x_scales, w1, w2, ka, p0, unit, w3, offs, nb1, nb2, nb3, out
):
    nc = tc.nc
    with ExitStack() as ctx:
        keep = ctx.enter_context(tc.tile_pool(name="keep", bufs=1))
        psum = ctx.enter_context(tc.psum_pool(name="psum", bufs=1))

        def tile(shape, dtype, name, on=""):
            return keep.tile(shape, dtype, name=name, tag=on, align_bytes=64)

        def bank(shape, b):
            return psum.tile(shape, F32, name="bank%d" % b)

        def load_list(src, name):
            entries = keep.tile([P, S // PER_COLUMN], U16, name=name)
            nc.sync.dma_start(entries[:], src)
            return entries

        def load_words(g):
            words = tile([P, T], I32, "x_words%d" % g)
            nc.sync.dma_start(out=words[:], in_=x_words[g].rearrange("p c r -> p (c r)").bitcast(I32))
            return words

        def load_rows(w, g, c0, c1, name):
            raw = tile([P, PACK, c1 - c0], F32, name)
            rows = w[g * P * PACK:(g + 1) * P * PACK, c0:c1]
            nc.sync.dma_start(out=raw[:], in_=rows.rearrange("(p t) c -> p t c", t=PACK))
            return raw

        x_planes = tile([P, T], U8, "x_planes")
        nc.gpsimd.memset(x_planes[:].bitcast(I32), 0)
        ident = tile([P, P], F32, "ident")
        make_identity(nc, ident[:])
        tanh_ar = [tile([P, S + SPARE], F32, "tanh_ar%d" % u) for u in range(TILES)]
        for u in range(TILES):
            nc.vector.memset(tanh_ar[u][:, S:], 0.0)

        factor_rows = tile([P, P], F32, "factor_rows")
        for n, factor in enumerate((ka, unit)):
            rows = factor.rearrange("(u p) o -> o u p", p=P).to_broadcast([P // 2 // TILES, TILES, P])
            nc.sync.dma_start(out=factor_rows[n * P // 2:(n + 1) * P // 2, :], in_=rows)
        x_table = [load_words(0)]
        picked = load_list(offs, "picked")
        for q in range(4):
            nc.sync.dma_start(out=x_planes[32 * q:32 * q + 4 * PASSES, :].bitcast(I32),
                              in_=x_scales[:, 4 * q:4 * q + 4, :].bitcast(I32))
        w2_raw = {(0, 0): load_rows(w2, 0, 0, PAIR, "w2_raw00")}
        x_table.append(load_words(1))
        w2_raw[0, 1] = load_rows(w2, 1, 0, PAIR, "w2_raw01")
        neighbours = [load_list(nb1, "nb1_list"), load_list(nb2, "nb2_list")]
        for g in range(PASSES):
            w2_raw[1, g] = load_rows(w2, g, PAIR, H, "w2_raw1%d" % g)
        neighbours.append(load_list(nb3, "nb3_list"))
        w1_raw = [load_rows(w1, g, 0, H, "w1_raw%d" % g) for g in range(PASSES)]
        w3_raw = load_rows(w3, 0, 0, N, "w3_raw")
        p0_pair = [tile([P, 2, S], F32, "p0_pair%d" % v) for v in range(2)]
        for v in range(2):
            nc.sync.dma_start(out=p0_pair[v][:], in_=p0[v * PAIR:(v + 1) * PAIR, :].rearrange("(r p) c -> p r c", p=P))

        def interleave(copy, raw, name):
            grouped = tile([P, raw.shape[2], PACK], BF16, name)
            copy(out=grouped[:].rearrange("p (c i) t -> p c t i", i=4),
                 in_=raw[:, :, :].rearrange("p t (c i) -> p c t i", i=4))
            return grouped

        def quantise(grouped, name):
            width = grouped.shape[1]
            codes = tile([P, width], U32, name + "_codes")
            scales = tile([P, width], U8, name + "_scales")
            nc.vector.quantize_mx(out=codes[:].bitcast(FP8X4), scales=scales[:],
                                  in_=grouped[:].rearrange("p c t -> p (c t)"))
            return codes, scales

        x_codes = [tile([P, S], U32, "x_codes%d" % g) for g in range(PASSES)]
        x_bytes = tile([P, S], U8, "x_bytes")

        def product(acc, weights, c0, g):
            codes, scales = weights
            nc.tensor.matmul_mx(
                out=acc[:], lhsT=codes[:, c0:c0 + P].bitcast(FP8X4), lhsT_scale=scales[:, c0:c0 + P],
                rhs=x_codes[g][:].bitcast(FP8X4), rhs_scale=x_bytes[4 * g:, :], start=(g == 0), stop=(g == PASSES - 1))

        factor_cols = bank([P, P], 5)
        nc.tensor.transpose(factor_cols[:], factor_rows[:], ident[:])
        near_mul = tile([P, TILES], F32, "near_mul")
        near_add = tile([P, TILES], F32, "near_add")
        unit_col = tile([P, TILES], F32, "unit_col")
        nc.scalar.activation(near_mul[:], factor_cols[:, :TILES], ACT.Copy, scale=0.5 * 0.333 / TENS)
        nc.scalar.activation(near_add[:], factor_cols[:, :TILES], ACT.Copy, scale=0.2 * 0.333 / TENS)
        nc.scalar.activation(unit_col[:], factor_cols[:, P // 2:P // 2 + TILES], ACT.Copy, scale=TENS)
        unit_spread = bank([P, TILES, P], 4)
        for u in range(TILES):
            nc.tensor.matmul(unit_spread[:, u, :], unit_col[:, u:u + 1].to_broadcast([P, P]), ident[:],
                             start=True, stop=True, is_transpose=True)
        unit_row = tile([P, 2, PAIR], F32, "unit_row")
        nc.scalar.copy(unit_row[:].rearrange("p v r -> p (v r)"), unit_spread[:].rearrange("p u r -> p (u r)"))

        near, own, sums = {}, {}, {}

        def area(u, weights, c0):
            acc = bank([P, S], u)
            for g in range(PASSES):
                product(acc, weights[g], c0, g)
            nc.scalar.activation(tanh_ar[u][:, :S], acc[:], ACT.Tanh)

        def make_near(u, on):
            near[u] = tile([P, S + SPARE], F32, "near%d" % u, on)
            nc.vector.tensor_scalar(near[u][:], tanh_ar[u][:], near_mul[:, u:u + 1], near_add[:, u:u + 1], ALU.mult, ALU.add)

        def make_own(u):
            own[u] = tile([P, S], F32, "own%d" % u)
            nc.vector.tensor_scalar(own[u][:], near[u][:, :S], -1.0 / 0.333, 0.8 * 1.5 / TENS, ALU.mult, ALU.add)

        def add_term(u, term, halves=BOTH_HALVES, last=False):
            v = u // 2
            for n, run in enumerate(RUNS[v]):
                if run[0] // 2 not in halves:
                    continue
                first = (v, n) not in sums
                if first:
                    sums[v, n] = bank([P, len(run), PAIR], SUM_BANK[v, n])
                for b, jb in enumerate(run):
                    c0 = (jb - 2 * halves[0]) * P
                    nc.tensor.matmul(sums[v, n][:, b, (u % 2) * P:(u % 2 + 1) * P], term[:, c0:c0 + P], ident[:],
                                     start=(first and b == 0), stop=(last and jb == run[-1]), is_transpose=True)

        def looked_up(u, i, halves):
            entries = neighbours[i][:, halves[0] * HALF // PER_COLUMN:(halves[-1] + 1) * HALF // PER_COLUMN]
            return near[u][:].indirect(entries)

        def fetch(u, i, halves=BOTH_HALVES, on=""):
            got = tile([P, HALF * len(halves)], F32, "got%d%d" % (u, i), on)
            nc.scalar.activation(got[:], looked_up(u, i, halves), ACT.Copy)
            return got[:]

        def fetch_with_own(u, halves=BOTH_HALVES, on=""):
            got = tile([P, HALF * len(halves)], F32, "got%d2" % u, on)
            plain = own[u][:, halves[0] * HALF:(halves[-1] + 1) * HALF]
            nc.vector.tensor_tensor(got[:], looked_up(u, 2, halves), plain, ALU.add)
            return got[:]

        hid_turned = [tile([P, 2, H], BF16, "hid_turned%d" % h) for h in range(2)]

        def close(v, n):
            run = RUNS[v][n]
            nc.vector.tensor_tensor(hid_turned[run[0] // 2][:, run[0] % 2:run[-1] % 2 + 1, v * PAIR:(v + 1) * PAIR],
                                    sums[v, n][:], unit_row[:, v:v + 1, :].to_broadcast([P, len(run), PAIR]), ALU.mult)

        def finish(n, back_bank, out_bank, copy):
            run = RUNS[1][n]
            cells = len(run) * P
            words = hid_turned[run[0] // 2][:].bitcast(F32)
            back = bank([P, len(run), 2, P], back_bank)
            for b, jb in enumerate(run):
                for e in range(2):
                    nc.tensor.transpose(back[:, b, e, :], words[:, jb % 2, e::2], ident[:])
            grouped = tile([P, cells, PACK], BF16, "hid_grouped%d" % n)
            copy(out=grouped[:].bitcast(F32).rearrange("p (b c) e -> p b c e", c=P), in_=back[:].rearrange("p b e c -> p b c e"))
            codes, scales = quantise(grouped, "hid%d" % n)
            acc = bank([P, N // P, cells], out_bank)
            for m in range(N // P):
                nc.tensor.matmul_mx(
                    out=acc[:, m, :], lhsT=w3_q[0][:, m * P:(m + 1) * P].bitcast(FP8X4), lhsT_scale=w3_q[1][:, m * P:(m + 1) * P],
                    rhs=codes[:].bitcast(FP8X4), rhs_scale=scales[:], start=True, stop=True)
            result = tile([P, N // P, cells], F32, "result%d" % n)
            copy(out=result[:], in_=acc[:])
            nc.sync.dma_start(out=out[:, run[0] * P:run[0] * P + cells].rearrange("(m p) c -> p m c", p=P), in_=result[:])

        nc.vector.tensor_copy(x_codes[0][:], x_table[0][:].bitcast(U32).indirect(picked[:]))
        nc.vector.tensor_copy(x_bytes[:], x_planes[:].indirect(picked[:]))
        nc.vector.tensor_copy(x_codes[1][:], x_table[1][:].bitcast(U32).indirect(picked[:]))
        codes, scales = quantise(interleave(nc.scalar.copy, w2_raw[0, 0], "w2_grouped00"), "w2_00")
        for u, copy in enumerate((nc.vector.tensor_copy, nc.scalar.copy)):
            second = quantise(interleave(copy, w2_raw[0, 1][:, :, u * P:(u + 1) * P], "w2_grouped01%d" % u), "w2_01%d" % u)
            area(u, [(codes[:, u * P:], scales[:, u * P:]), second], 0)

        w2_q, w1_q = [], []
        for g in range(PASSES):
            grouped = interleave(nc.vector.tensor_copy, w2_raw[1, g], "w2_grouped1%d" % g)
            make_near(g, on="w2_raw1%d" % g)
            w2_q.append(quantise(grouped, "w2_1%d" % g))
            make_own(g)
        area(2, w2_q, 0)
        area(3, w2_q, P)
        got00 = fetch(0, 0)
        got01 = fetch(0, 1)
        for g in range(PASSES):
            grouped = interleave(nc.vector.tensor_copy, w1_raw[g], "w1_grouped%d" % g)
            make_near(2 + g, on="w1_raw%d" % g)
            w1_q.append(quantise(grouped, "w1_%d" % g))
            make_own(2 + g)

        got02 = fetch(0, 2, on="w2_11_scales")
        for term in (own[0][:], got00, got01):
            add_term(0, term)
        pr = [bank([P, S], TILES + u) for u in range(TILES)]
        for u in range(TILES):
            for g in range(PASSES):
                product(pr[u], w1_q[g], u * P, g)
        got10 = fetch(1, 0, on="tanh_ar2")
        got11 = fetch(1, 1, on="got00")
        got12 = fetch_with_own(1, on="tanh_ar3")
        for u, term in ((0, got02), (1, got12), (1, got11), (1, got10)):
            add_term(u, term)
        w3_q = quantise(interleave(nc.scalar.copy, w3_raw, "w3_grouped"), "w3")
        for u in range(TILES):
            tanh_pr = tile([P, S], F32, "tanh_pr%d" % u)
            nc.scalar.activation(tanh_pr[:], pr[u][:], ACT.Tanh)
            tension = tile([P, S], F32, "tension%d" % u)
            nc.vector.scalar_tensor_tensor(tension[:], p0_pair[u // 2][:, u % 2, :], -0.8 / TENS, tanh_pr[:], ALU.mult, ALU.add)
            add_term(u, tension[:], last=(u == 1))

        add_term(2, fetch(2, 0, FIRST_HALF, on="w1_1_codes"), FIRST_HALF)
        add_term(2, fetch(2, 1, FIRST_HALF, on="w1_1_scales"), FIRST_HALF)
        add_term(2, fetch_with_own(2, FIRST_HALF, on="tanh_pr2"), FIRST_HALF)
        add_term(3, fetch_with_own(3, FIRST_HALF, on="tanh_pr3"), FIRST_HALF)
        close(0, 0)
        add_term(3, fetch(3, 0, FIRST_HALF, on="tanh_pr0"), FIRST_HALF)
        add_term(3, fetch(3, 1, FIRST_HALF, on="tanh_pr1"), FIRST_HALF, last=True)
        close(1, 0)
        close(0, 1)
        add_term(2, fetch(2, 0, SECOND_HALF, on="w1_1_codes"), SECOND_HALF)
        add_term(2, fetch(2, 1, SECOND_HALF, on="w1_1_scales"), SECOND_HALF)
        finish(0, back_bank=5, out_bank=6, copy=nc.scalar.copy)
        add_term(2, fetch_with_own(2, SECOND_HALF, on="tanh_pr2"), SECOND_HALF)
        add_term(3, fetch(3, 0, SECOND_HALF, on="tanh_pr0"), SECOND_HALF)
        add_term(3, fetch_with_own(3, SECOND_HALF, on="tanh_pr3"), SECOND_HALF)
        add_term(3, fetch(3, 1, SECOND_HALF, on="tanh_pr1"), SECOND_HALF, last=True)
        close(1, 1)
        close(1, 2)
        finish(1, back_bank=2, out_bank=3, copy=nc.scalar.copy)
        finish(2, back_bank=7, out_bank=0, copy=nc.vector.tensor_copy)
